import numpy as np
import ml_dtypes


def mxq(x, axis, fmt="e4m3"):
    dtype, down = {"e4m3": (ml_dtypes.float8_e4m3fn, 7), "e5m2": (ml_dtypes.float8_e5m2, 14)}[fmt]
    v = np.moveaxis(np.asarray(x, np.float32).astype(ml_dtypes.bfloat16).astype(np.float64), axis, -1)
    blocks = v.reshape(v.shape[:-1] + (-1, 32))
    amax = np.abs(blocks).max(-1, keepdims=True)
    byte = np.maximum(np.where(amax > 0, np.frexp(amax)[1] - 1 + 127, 0) - down, 1)
    scale = np.exp2(byte - 127.0)
    codes = (blocks / scale).astype(np.float32).astype(dtype).astype(np.float64)
    return np.moveaxis((codes * scale).reshape(v.shape), -1, axis)


WIDE = False


def mx_kscale(k):
    if not WIDE:
        return np.ones(k)
    levels = np.array([10, -10, 5, -5, 0])
    if k % 512:
        return np.exp2(np.random.permutation(np.resize(levels, k // 32))).repeat(32)
    a = np.empty((k // 512, 16))
    for p in range(k // 512):
        a[p, :8] = np.random.permutation(np.resize(levels, 8))
        for g in range(8):
            far = levels[np.abs(levels - a[p, g]) >= 10]
            a[p, g + 8] = far[np.random.randint(len(far))]
    return np.exp2(a.ravel()).repeat(32)


def f64(x):
    return np.asarray(x).astype(np.float64)


def striped(idx):
    return np.tile(np.asarray(idx).reshape(-1, 16).T, (8, 1)).astype(np.uint16)


def unstriped(offs):
    return offs[:16].T.reshape(-1).astype(np.int64)


E2M1 = np.array([0.0, 0.5, 1.0, 1.5, 2.0, 3.0, 4.0, 6.0, -0.0, -0.5, -1.0, -1.5, -2.0, -3.0, -4.0, -6.0])


def pack_weight(w, fmt):
    k, n = w.shape
    w = f64(np.asarray(w, np.float32).astype(ml_dtypes.bfloat16)).reshape(k // 32, 32, n)
    amax = np.abs(w).max(1)
    if fmt == "e4m3":
        byte = np.frexp(amax)[1] - 1 + 127 - 7
    else:
        mant, ex = np.frexp(amax / 6.0)
        byte = np.where(mant > 0.5, ex, ex - 1) + 127
    byte = np.clip(np.where(amax > 0, byte, 1), 1, 254)
    scaled = (w * np.exp2(127.0 - byte)[:, None, :]).reshape(k, n).astype(np.float32)
    by_word = np.ascontiguousarray(scaled.reshape(k // 512, 128, 4, n).transpose(0, 1, 3, 2))
    if fmt == "e4m3":
        words = by_word.astype(ml_dtypes.float8_e4m3fn).view(np.uint8)
    else:
        c = by_word.astype(ml_dtypes.float4_e2m1fn).view(np.uint8) & 0xF
        words = (c[..., 0::2] | (c[..., 1::2] << 4)).reshape(k // 512, 128, 2 * n)
    return np.ascontiguousarray(words), np.ascontiguousarray(byte.astype(np.uint8).reshape(k // 512, 16, n))


def unpack_weight(words, scales, fmt):
    g, _, n = scales.shape
    words = np.ascontiguousarray(words).reshape(g, 128, n, -1)
    if fmt == "e4m3":
        vals = words.view(ml_dtypes.float8_e4m3fn).astype(np.float64)
    else:
        nib = np.empty((g, 128, n, 4), np.uint8)
        nib[..., 0::2] = words & 0xF
        nib[..., 1::2] = words >> 4
        vals = E2M1[nib]
    vals = vals * np.repeat(np.exp2(scales.astype(np.float64) - 127.0), 8, axis=1)[..., None]
    return vals.transpose(0, 1, 3, 2).reshape(g * 512, n)


def bf(x):
    return np.asarray(x, np.float32).astype(ml_dtypes.bfloat16)


def planes(Y):
    r, m = Y.shape
    b = f64(bf(Y)).reshape(r // 32, 32, m)
    amax = np.abs(b).max(1)
    byte = np.clip(np.where(amax > 0, np.frexp(amax)[1] - 1 + 127 - 7, 1), 1, 254)
    codes = (b * np.exp2(127.0 - byte)[:, None, :]).reshape(r, m).astype(np.float32).astype(ml_dtypes.float8_e4m3fn).view(np.uint8)
    words = codes.reshape(r // 512, 128, 4, m).transpose(0, 1, 3, 2)
    return np.ascontiguousarray(words), np.ascontiguousarray(byte.astype(np.uint8).reshape(r // 512, 16, m))


D, T, I, Q, E, Z, X = 512, 2048, 512, 256, 512, 1024, 1024


def setup_inputs():
    n = np.random.standard_normal
    idx = np.random.permutation(T)[:I]
    idx2 = np.random.permutation(Z)[:I]
    idx3 = np.random.permutation(Z)[:I]
    idx4 = np.random.permutation(X)[:I]
    fd = mx_kscale(D)
    fi = mx_kscale(I)
    keysp = pack_weight(n((D, T)) / fd[:, None], "e2m1")
    return {
        "query": (n((D, Q)) * 1.0 / np.sqrt(D) * fd[:, None]).astype(np.float32),
        "keys_words": keysp[0],
        "keys_scales": keysp[1],
        "os": (np.random.uniform(0.02, 0.08, (1, I)) * fi).astype(np.float32),
        "vals": (n((E, T))).astype(np.float32),
        "vals2": (n((E, X))).astype(np.float32),
        "vsc": (np.random.uniform(0.5, 2.0, (1, I)) / fi).astype(np.float32),
        "offs": striped(idx),
        "offs2": striped(idx2),
        "offs3": striped(idx3),
        "offs4": striped(idx4),
    }


def reference(query, keys_words, keys_scales, os, vals, vals2, vsc, offs, offs2, offs3, offs4):
    idx = unstriped(offs)
    idx2 = unstriped(offs2)
    idx3 = unstriped(offs3)
    idx4 = unstriped(offs4)
    keysu = unpack_weight(keys_words, keys_scales, "e2m1")
    queryq = mxq(f64(query), 0, "e4m3")
    keysidxg = keysu[:, idx]
    a = queryq.T @ keysidxg
    f0 = np.zeros((Q, Z))
    f0[:, idx2] = a
    w = a + f0[:, idx3]
    wo1 = w * f64(os)
    wt1 = wo1.T
    vz = np.maximum(f64(vals)[:, idx], f64(vals2)[:, idx4]) * f64(vsc)
    vt1 = vz.T
    vt1q = mxq(vt1, 0, "e4m3")
    wt1q = mxq(wt1, 0, "e4m3")
    o = vt1q.T @ wt1q
    words, scales = planes(o)
    return o, words, scales

@@ -1,0 +1,259 @@
+from contextlib import ExitStack
+
+import concourse.mybir as mybir
+from concourse.masks import make_identity
+
+D, T, I, Q, E, Z, X = 512, 2048, 512, 256, 512, 1024, 1024
+FLOPS = 2 * D * Q * I + 2 * I * E * Q
+
+F32 = mybir.dt.float32
+BF16 = mybir.dt.bfloat16
+I32 = mybir.dt.int32
+U32 = mybir.dt.uint32
+U16 = mybir.dt.uint16
+U8 = mybir.dt.uint8
+FP8X4 = mybir.dt.float8_e4m3fn_x4
+FP4X4 = mybir.dt.float4_e2m1fn_x4
+COPY = mybir.ActivationFunctionType.Copy
+ADD = mybir.AluOpType.add
+MULT = mybir.AluOpType.mult
+MAX = mybir.AluOpType.max
+
+P = 128
+PACK = 4
+RUN = 8
+HALVES = Q // P
+LIST_COLS = I // 16
+
+
+def dealt(ap):
+    return ap.rearrange("p (b t r) -> p t b r", t=PACK, r=RUN)
+
+
+def tile_attend_passedthrough_mergedvalues_lean_pl_kernel(
+    tc, query, keys_words, keys_scales, w_factor, vals, vals2, v_factor, offs, offs2, offs3, offs4, out_0, out_1, out_2
+):
+    nc = tc.nc
+    with ExitStack() as ctx:
+        keep = ctx.enter_context(tc.tile_pool(name="keep", bufs=1))
+        psum = ctx.enter_context(tc.psum_pool(name="psum", bufs=1))
+
+        def tile(name, shape, dtype, tag=None):
+            return keep.tile(shape, dtype, name=name, tag=tag or name, align_bytes=64)
+
+        key_list = tile("key_list", [P, LIST_COLS], U16)
+        put_list = tile("put_list", [P, LIST_COLS], U16)
+        get_list = tile("get_list", [P, LIST_COLS], U16)
+        second_list = tile("second_list", [P, LIST_COLS], U16)
+        pool_words = tile("pool_words", [P, T], U16)
+        pool_scales = tile("pool_scales", [P, T], U8)
+        q_raw = tile("q_raw", [P, PACK, Q], F32)
+        first = [tile(f"first{t}", [P, T], F32) for t in range(PACK)]
+        second = [tile(f"second{t}", [P, X], F32) for t in range(PACK)]
+        places = [tile(f"places{h}", [P, Z], F32) for h in range(HALVES)]
+        factor_rows = tile("factor_rows", [P, P], F32)
+        factors = tile("factors", [P, 2 * PACK], F32)
+        ident = tile("ident", [P, P], F32)
+
+        nc.vector.memset(pool_scales[:].bitcast(I32), 0)
+        for h in range(HALVES):
+            nc.vector.memset(places[h][:], 0.0)
+        nc.gpsimd.memset(factor_rows[:], 0.0)
+        make_identity(nc, ident[:])
+
+        vals_rows = vals.rearrange("(p t) c -> p t c", t=PACK)
+        vals2_rows = vals2.rearrange("(p t) c -> p t c", t=PACK)
+        nc.sync.dma_start(key_list[:], offs)
+        nc.sync.dma_start(second_list[:], offs4)
+        nc.sync.dma_start(out=pool_words[:].bitcast(I32), in_=keys_words[0].bitcast(I32))
+        for quad in range(4):
+            nc.scalar.dma_start(
+                out=pool_scales[32 * quad : 32 * quad + 4, :].bitcast(I32),
+                in_=keys_scales[0, 4 * quad : 4 * quad + 4, :].bitcast(I32),
+            )
+        nc.sync.dma_start(out=q_raw[:], in_=query.rearrange("(p j) q -> p j q", j=PACK))
+        nc.sync.dma_start(out=second[0][:], in_=vals2_rows[:, 0, :])
+        for n, vec in enumerate((w_factor, v_factor)):
+            nc.sync.dma_start(
+                out=factor_rows[PACK * n : PACK * (n + 1), :].rearrange("t (b r) -> t b r", r=RUN),
+                in_=vec[0].rearrange("(b t r) -> t b r", t=PACK, r=RUN),
+            )
+        nc.sync.dma_start(out=second[1][:], in_=vals2_rows[:, 1, :])
+        nc.sync.dma_start(put_list[:], offs2)
+        nc.sync.dma_start(out=first[0][:], in_=vals_rows[:, 0, :])
+        nc.sync.dma_start(get_list[:], offs3)
+        nc.sync.dma_start(out=first[1][:], in_=vals_rows[:, 1, :])
+        nc.sync.dma_start(out=second[2][:], in_=vals2_rows[:, 2, :])
+        for t in (2, 3):
+            nc.sync.dma_start(out=first[t][:], in_=vals_rows[:, t, :])
+        nc.sync.dma_start(out=second[3][:], in_=vals2_rows[:, 3, :])
+
+        key_scales = tile("key_scales", [P, I], U8)
+        key_words = tile("key_words", [P, I], U16)
+        nc.vector.tensor_copy(key_scales[:], pool_scales[:].indirect(key_list[:]))
+        nc.vector.tensor_copy(key_words[:], pool_words[:].indirect(key_list[:]))
+
+        def quantise(name, src, width):
+            codes = tile(name + "_codes", [P, width], U32)
+            scales = tile(name + "_scales", [P, width], U8)
+            nc.vector.quantize_mx(out=codes[:].bitcast(FP8X4), scales=scales[:], in_=src)
+            return codes, scales
+
+        score_banks, scores = [], []
+        for h in range(HALVES):
+            q_bf = tile(f"q_bf{h}", [P, P, PACK], BF16)
+            nc.scalar.activation(
+                q_bf[:].rearrange("p (c i) t -> p c t i", i=4),
+                q_raw[:, :, P * h : P * (h + 1)].rearrange("p t (c i) -> p c t i", i=4),
+                COPY,
+            )
+            q_codes, q_scales = quantise(f"q{h}", q_bf[:].rearrange("p q t -> p (q t)"), P)
+            bank = psum.tile([P, I], F32, name=f"score_bank{h}", tag=f"half{h}")
+            nc.tensor.matmul_mx(
+                out=bank[:],
+                lhsT=q_codes[:].bitcast(FP8X4),
+                lhsT_scale=q_scales[:],
+                rhs=key_words[:].bitcast(FP4X4),
+                rhs_scale=key_scales[:],
+                start=True,
+                stop=True,
+            )
+            score_banks.append(bank)
+
+        first_g = [tile(f"first_g{t}", [P, I], F32) for t in range(PACK)]
+        second_g = [tile(f"second_g{t}", [P, I], F32) for t in range(PACK)]
+
+        def gather_scalar(dst, window, offsets):
+            nc.scalar.activation(dst[:], window[:].indirect(offsets[:]), COPY)
+
+        def gather_vector(dst, window, offsets):
+            nc.vector.tensor_copy(dst[:], window[:].indirect(offsets[:]))
+
+        gather_scalar(second_g[0], second[0], second_list)
+        gather_vector(second_g[1], second[1], second_list)
+
+        for h in range(HALVES):
+            score = tile(f"score{h}", [P, I], F32)
+            nc.scalar.copy(score[:], score_banks[h][:])
+            scores.append(score)
+
+        factor_bank = psum.tile([P, P], F32, name="factor_bank")
+        nc.tensor.transpose(factor_bank[:], factor_rows[:], ident[:])
+        nc.scalar.copy(factors[:], factor_bank[:, 0 : 2 * PACK])
+
+        nc.vector.tensor_copy(places[0][:].indirect(put_list[:]), scores[0][:])
+        for part in range(2):
+            nc.scalar.activation(
+                places[1][:].indirect(put_list[:, 16 * part : 16 * (part + 1)]),
+                scores[1][:, 256 * part : 256 * (part + 1)],
+                COPY,
+            )
+
+        looked = [tile(f"looked{h}", [P, I], F32) for h in range(HALVES)]
+        gather_vector(first_g[0], first[0], key_list)
+        gather_scalar(looked[0], places[0], get_list)
+        gather_vector(looked[1], places[1], get_list)
+
+        def turn(name, tag, src, bufs):
+            bank = psum.tile([P, PACK, P], F32, name=name, tag=tag, bufs=bufs)
+            for t in range(PACK):
+                nc.tensor.transpose(bank[:, t, :], src[:, t, :], ident[:])
+            return bank
+
+        def scale_round(name, bank, column, tag=None):
+            rounded = tile(name, [P, P, PACK], BF16, tag)
+            nc.vector.tensor_tensor(
+                rounded[:],
+                bank[:].rearrange("p t c -> p c t"),
+                factors[:, column : column + PACK].unsqueeze(1).to_broadcast([P, P, PACK]),
+                MULT,
+            )
+            return rounded
+
+        def merge(t, parts=1):
+            merged = tile(f"merged{t}", [P, PACK, P], F32)
+            step = PACK // parts
+            for j in range(0, PACK, step):
+                nc.vector.tensor_tensor(
+                    merged[:, j : j + step, :].rearrange("p t (b r) -> p t b r", r=RUN),
+                    dealt(first_g[t][:])[:, j : j + step],
+                    dealt(second_g[t][:])[:, j : j + step],
+                    MAX,
+                )
+            return turn(f"v_bank{t}", "v_bank", merged, 3)
+
+        v_banks = [merge(0)]
+        w_banks = []
+        for h in range(HALVES):
+            weights = tile(f"weights{h}", [P, PACK, P], F32)
+            nc.vector.tensor_tensor(
+                weights[:].rearrange("p t (b r) -> p t b r", r=RUN), dealt(looked[h][:]), dealt(score_banks[h][:]), ADD
+            )
+            w_banks.append(turn(f"w_bank{h}", f"half{h}", weights, 1))
+
+        v_bf = [scale_round("v_bf0", v_banks[0], PACK)]
+        w_bf = [scale_round(f"w_bf{h}", w_banks[h], 0) for h in range(HALVES)]
+        gather_scalar(first_g[1], first[1], key_list)
+        v_banks.append(merge(1))
+        w_q = [quantise(f"w{h}", w_bf[h][:].rearrange("p q t -> p (q t)"), P) for h in range(HALVES)]
+
+        out_banks = [psum.tile([P, PACK, P], F32, name=f"out_bank{h}") for h in range(HALVES)]
+
+        def product(t):
+            v_codes, v_scales = quantise(f"v{t}", v_bf[t][:].rearrange("p e t -> p (e t)"), P)
+            for h in range(HALVES):
+                nc.tensor.matmul_mx(
+                    out=out_banks[h][:, t, :],
+                    lhsT=v_codes[:].bitcast(FP8X4),
+                    lhsT_scale=v_scales[:],
+                    rhs=w_q[h][0][:].bitcast(FP8X4),
+                    rhs_scale=w_q[h][1][:],
+                    start=True,
+                    stop=True,
+                )
+
+        product(0)
+        gather_scalar(second_g[2], second[2], second_list)
+        gather_scalar(first_g[2], first[2], key_list)
+        v_banks.append(merge(2))
+        v_bf.append(scale_round("v_bf1", v_banks[1], PACK, "first_g2"))
+        product(1)
+        gather_scalar(first_g[3], first[3], key_list)
+        gather_scalar(second_g[3], second[3], second_list)
+
+        result = tile("result", [P, PACK, Q], F32, "second3")
+        out_rows = out_0.rearrange("(p t) q -> p t q", t=PACK)
+        for h in range(HALVES):
+            nc.scalar.copy(result[:, 0:2, P * h : P * (h + 1)], out_banks[h][:, 0:2, :])
+        nc.sync.dma_start(out=out_rows[:, 0:2, :], in_=result[:, 0:2, :])
+
+        v_banks.append(merge(3, 2))
+        v_bf.append(scale_round("v_bf2", v_banks[2], PACK, "first_g3"))
+        product(2)
+        v_bf.append(scale_round("v_bf3", v_banks[3], PACK))
+        product(3)
+
+        out_bf = [tile(f"out_bf{h}", [P, P, PACK], BF16) for h in range(HALVES)]
+        nc.vector.tensor_copy(out_bf[0][:], out_banks[0][:].rearrange("p t q -> p q t"))
+        nc.scalar.copy(out_bf[1][:], out_banks[1][:].rearrange("p t q -> p q t"))
+        out_codes = tile("out_codes", [P, Q], U32)
+        out_scales = tile("out_scales", [P, Q], U8)
+        for h in range(HALVES):
+            cols = slice(P * h, P * (h + 1))
+            nc.vector.quantize_mx(
+                out=out_codes[:, cols].bitcast(FP8X4),
+                scales=out_scales[:, cols],
+                in_=out_bf[h][:].rearrange("p q t -> p (q t)"),
+            )
+        for h in (1, 0):
+            nc.scalar.copy(result[:, 2:4, P * h : P * (h + 1)], out_banks[h][:, 2:4, :])
+        nc.scalar.dma_start(out=out_rows[:, 2:4, :], in_=result[:, 2:4, :])
+        nc.sync.dma_start(
+            out=out_1[0].rearrange("p c r -> p (c r)").bitcast(I32), in_=out_codes[:].bitcast(I32)
+        )
+        for quad in range(4):
+            queue = nc.sync if quad < 2 else nc.scalar
+            queue.dma_start(
+                out=out_2[0, 4 * quad : 4 * quad + 4, :].bitcast(I32),
+                in_=out_scales[32 * quad : 32 * quad + 4, :].bitcast(I32),
+            )

@@ -51,33 +51,31 @@ def tile_attend_passedthrough_mergedvalues_lean_pl_kernel(
         first = [tile(f"first{t}", [P, T], F32) for t in range(PACK)]
         second = [tile(f"second{t}", [P, X], F32) for t in range(PACK)]
         places = [tile(f"places{h}", [P, Z], F32) for h in range(HALVES)]
-        factor_rows = tile("factor_rows", [P, P], F32)
-        factors = tile("factors", [P, 2 * PACK], F32)
+        factor_in = tile("factor_in", [2, I], F32)
+        factor_rows = tile("factor_rows", [P, PACK, P], F32)
+        factors = tile("factors", [P, 2, PACK], F32)
         ident = tile("ident", [P, P], F32)
 
-        nc.vector.memset(pool_scales[:].bitcast(I32), 0)
+        nc.gpsimd.memset(pool_scales[:].bitcast(I32), 0)
         for h in range(HALVES):
             nc.vector.memset(places[h][:], 0.0)
-        nc.gpsimd.memset(factor_rows[:], 0.0)
+        nc.vector.memset(factor_rows[:], 0.0)
+        for n, vec in enumerate((w_factor, v_factor)):
+            nc.scalar.dma_start(out=factor_in[n : n + 1, :], in_=vec)
         make_identity(nc, ident[:])
 
         vals_rows = vals.rearrange("(p t) c -> p t c", t=PACK)
         vals2_rows = vals2.rearrange("(p t) c -> p t c", t=PACK)
         nc.sync.dma_start(key_list[:], offs)
-        nc.sync.dma_start(second_list[:], offs4)
         nc.sync.dma_start(out=pool_words[:].bitcast(I32), in_=keys_words[0].bitcast(I32))
         for quad in range(4):
-            nc.scalar.dma_start(
+            nc.sync.dma_start(
                 out=pool_scales[32 * quad : 32 * quad + 4, :].bitcast(I32),
                 in_=keys_scales[0, 4 * quad : 4 * quad + 4, :].bitcast(I32),
             )
+        nc.sync.dma_start(second_list[:], offs4)
         nc.sync.dma_start(out=q_raw[:], in_=query.rearrange("(p j) q -> p j q", j=PACK))
         nc.sync.dma_start(out=second[0][:], in_=vals2_rows[:, 0, :])
-        for n, vec in enumerate((w_factor, v_factor)):
-            nc.sync.dma_start(
-                out=factor_rows[PACK * n : PACK * (n + 1), :].rearrange("t (b r) -> t b r", r=RUN),
-                in_=vec[0].rearrange("(b t r) -> t b r", t=PACK, r=RUN),
-            )
         nc.sync.dma_start(out=second[1][:], in_=vals2_rows[:, 1, :])
         nc.sync.dma_start(put_list[:], offs2)
         nc.sync.dma_start(out=first[0][:], in_=vals_rows[:, 0, :])
@@ -87,6 +85,16 @@ def tile_attend_passedthrough_mergedvalues_lean_pl_kernel(
         for t in (2, 3):
             nc.sync.dma_start(out=first[t][:], in_=vals_rows[:, t, :])
         nc.sync.dma_start(out=second[3][:], in_=vals2_rows[:, 3, :])
+
+        def turn(name, tag, src, bufs):
+            bank = psum.tile([P, PACK, P], F32, name=name, tag=tag, bufs=bufs)
+            for t in range(PACK):
+                nc.tensor.transpose(bank[:, t, :], src[:, t, :], ident[:])
+            return bank
+
+        nc.vector.tensor_copy(factor_rows[0:2].rearrange("p t (b r) -> p t b r", r=RUN), dealt(factor_in[:]))
+        factor_bank = turn("factor_bank", "factor_bank", factor_rows, 1)
+        nc.scalar.activation(factors[:], factor_bank[:, :, 0:2].rearrange("p t n -> p n t"), COPY)
 
         key_scales = tile("key_scales", [P, I], U8)
         key_words = tile("key_words", [P, I], U16)
@@ -121,7 +129,7 @@ def tile_attend_passedthrough_mergedvalues_lean_pl_kernel(
             score_banks.append(bank)
 
         first_g = [tile(f"first_g{t}", [P, I], F32) for t in range(PACK)]
-        second_g = [tile(f"second_g{t}", [P, I], F32) for t in range(PACK)]
+        second_g = [tile(f"second_g{t}", [P, I], F32, "q_raw" if t == 1 else None) for t in range(PACK)]
 
         def gather_scalar(dst, window, offsets):
             nc.scalar.activation(dst[:], window[:].indirect(offsets[:]), COPY)
@@ -137,10 +145,6 @@ def tile_attend_passedthrough_mergedvalues_lean_pl_kernel(
             nc.scalar.copy(score[:], score_banks[h][:])
             scores.append(score)
 
-        factor_bank = psum.tile([P, P], F32, name="factor_bank")
-        nc.tensor.transpose(factor_bank[:], factor_rows[:], ident[:])
-        nc.scalar.copy(factors[:], factor_bank[:, 0 : 2 * PACK])
-
         nc.vector.tensor_copy(places[0][:].indirect(put_list[:]), scores[0][:])
         for part in range(2):
             nc.scalar.activation(
@@ -154,24 +158,16 @@ def tile_attend_passedthrough_mergedvalues_lean_pl_kernel(
         gather_scalar(looked[0], places[0], get_list)
         gather_vector(looked[1], places[1], get_list)
 
-        def turn(name, tag, src, bufs):
-            bank = psum.tile([P, PACK, P], F32, name=name, tag=tag, bufs=bufs)
-            for t in range(PACK):
-                nc.tensor.transpose(bank[:, t, :], src[:, t, :], ident[:])
-            return bank
-
-        def scale_round(name, bank, column, tag=None):
-            rounded = tile(name, [P, P, PACK], BF16, tag)
+        def scale_round(rounded, bank, column):
             nc.vector.tensor_tensor(
-                rounded[:],
+                rounded,
                 bank[:].rearrange("p t c -> p c t"),
-                factors[:, column : column + PACK].unsqueeze(1).to_broadcast([P, P, PACK]),
+                factors[:, column : column + 1, :].to_broadcast([P, P, PACK]),
                 MULT,
             )
             return rounded
 
-        def merge(t, parts=1):
-            merged = tile(f"merged{t}", [P, PACK, P], F32)
+        def merge(t, merged, parts=1):
             step = PACK // parts
             for j in range(0, PACK, step):
                 nc.vector.tensor_tensor(
@@ -182,25 +178,32 @@ def tile_attend_passedthrough_mergedvalues_lean_pl_kernel(
                 )
             return turn(f"v_bank{t}", "v_bank", merged, 3)
 
-        v_banks = [merge(0)]
+        def fresh(name, tag=None):
+            return tile(name, [P, PACK, P], F32, tag)[:]
+
+        def fresh_bf(name, tag=None):
+            return tile(name, [P, P, PACK], BF16, tag)[:]
+
+        pair = tile("pair", [P, 2, PACK, P], F32, "places0")
+        v_banks = [merge(0, pair[:, 0])]
         w_banks = []
         for h in range(HALVES):
-            weights = tile(f"weights{h}", [P, PACK, P], F32)
+            weights = fresh("weights0") if h == 0 else pair[:, 1]
             nc.vector.tensor_tensor(
-                weights[:].rearrange("p t (b r) -> p t b r", r=RUN), dealt(looked[h][:]), dealt(score_banks[h][:]), ADD
+                weights.rearrange("p t (b r) -> p t b r", r=RUN), dealt(looked[h][:]), dealt(score_banks[h][:]), ADD
             )
             w_banks.append(turn(f"w_bank{h}", f"half{h}", weights, 1))
 
-        v_bf = [scale_round("v_bf0", v_banks[0], PACK)]
-        w_bf = [scale_round(f"w_bf{h}", w_banks[h], 0) for h in range(HALVES)]
+        v_bf = [scale_round(fresh_bf("v_bf0"), v_banks[0], 1)]
+        w_bf = [scale_round(fresh_bf(f"w_bf{h}"), w_banks[h], 0) for h in range(HALVES)]
         gather_scalar(first_g[1], first[1], key_list)
-        v_banks.append(merge(1))
-        w_q = [quantise(f"w{h}", w_bf[h][:].rearrange("p q t -> p (q t)"), P) for h in range(HALVES)]
+        v_banks.append(merge(1, fresh("merged1")))
+        w_q = [quantise(f"w{h}", w_bf[h].rearrange("p q t -> p (q t)"), P) for h in range(HALVES)]
 
         out_banks = [psum.tile([P, PACK, P], F32, name=f"out_bank{h}") for h in range(HALVES)]
 
         def product(t):
-            v_codes, v_scales = quantise(f"v{t}", v_bf[t][:].rearrange("p e t -> p (e t)"), P)
+            v_codes, v_scales = quantise(f"v{t}", v_bf[t].rearrange("p e t -> p (e t)"), P)
             for h in range(HALVES):
                 nc.tensor.matmul_mx(
                     out=out_banks[h][:, t, :],
@@ -215,22 +218,25 @@ def tile_attend_passedthrough_mergedvalues_lean_pl_kernel(
         product(0)
         gather_scalar(second_g[2], second[2], second_list)
         gather_scalar(first_g[2], first[2], key_list)
-        v_banks.append(merge(2))
-        v_bf.append(scale_round("v_bf1", v_banks[1], PACK, "first_g2"))
+        v_banks.append(merge(2, fresh("merged2")))
+        v_bf.append(scale_round(fresh_bf("v_bf1", "first2"), v_banks[1], 1))
         product(1)
         gather_scalar(first_g[3], first[3], key_list)
         gather_scalar(second_g[3], second[3], second_list)
 
-        result = tile("result", [P, PACK, Q], F32, "second3")
+        late = tile("late", [P, X], F32, "second3")
+        early_rows = late[:, 0 : 2 * Q].rearrange("p (t q) -> p t q", t=2)
+        late_bf = late[:, 2 * Q : 3 * Q].bitcast(BF16).rearrange("p (e t) -> p e t", t=PACK)
+        last_rows = tile("last_rows", [P, 2, Q], F32)
         out_rows = out_0.rearrange("(p t) q -> p t q", t=PACK)
         for h in range(HALVES):
-            nc.scalar.copy(result[:, 0:2, P * h : P * (h + 1)], out_banks[h][:, 0:2, :])
-        nc.sync.dma_start(out=out_rows[:, 0:2, :], in_=result[:, 0:2, :])
+            nc.scalar.copy(early_rows[:, :, P * h : P * (h + 1)], out_banks[h][:, 0:2, :])
+        nc.sync.dma_start(out=out_rows[:, 0:2, :], in_=early_rows)
 
-        v_banks.append(merge(3, 2))
-        v_bf.append(scale_round("v_bf2", v_banks[2], PACK, "first_g3"))
+        v_banks.append(merge(3, fresh("merged3"), 2))
+        v_bf.append(scale_round(late_bf, v_banks[2], 1))
         product(2)
-        v_bf.append(scale_round("v_bf3", v_banks[3], PACK))
+        v_bf.append(scale_round(fresh_bf("v_bf3"), v_banks[3], 1))
         product(3)
 
         out_bf = [tile(f"out_bf{h}", [P, P, PACK], BF16) for h in range(HALVES)]
@@ -246,8 +252,8 @@ def tile_attend_passedthrough_mergedvalues_lean_pl_kernel(
                 in_=out_bf[h][:].rearrange("p q t -> p (q t)"),
             )
         for h in (1, 0):
-            nc.scalar.copy(result[:, 2:4, P * h : P * (h + 1)], out_banks[h][:, 2:4, :])
-        nc.scalar.dma_start(out=out_rows[:, 2:4, :], in_=result[:, 2:4, :])
+            nc.scalar.copy(last_rows[:, :, P * h : P * (h + 1)], out_banks[h][:, 2:4, :])
+        nc.scalar.dma_start(out=out_rows[:, 2:4, :], in_=last_rows[:])
         nc.sync.dma_start(
             out=out_1[0].rearrange("p c r -> p (c r)").bitcast(I32), in_=out_codes[:].bitcast(I32)
         )

@@ -110,11 +110,7 @@ def tile_attend_passedthrough_mergedvalues_lean_pl_kernel(
         score_banks, scores = [], []
         for h in range(HALVES):
             q_bf = tile(f"q_bf{h}", [P, P, PACK], BF16)
-            nc.scalar.activation(
-                q_bf[:].rearrange("p (c i) t -> p c t i", i=4),
-                q_raw[:, :, P * h : P * (h + 1)].rearrange("p t (c i) -> p c t i", i=4),
-                COPY,
-            )
+            nc.scalar.activation(q_bf[:], q_raw[:, :, P * h : P * (h + 1)].rearrange("p t q -> p q t"), COPY)
             q_codes, q_scales = quantise(f"q{h}", q_bf[:].rearrange("p q t -> p (q t)"), P)
             bank = psum.tile([P, I], F32, name=f"score_bank{h}", tag=f"half{h}")
             nc.tensor.matmul_mx(

from contextlib import ExitStack

import concourse.mybir as mybir
from concourse.masks import make_identity

D, T, I, Q, E, Z, X = 512, 2048, 512, 256, 512, 1024, 1024
FLOPS = 2 * D * Q * I + 2 * I * E * Q

F32 = mybir.dt.float32
BF16 = mybir.dt.bfloat16
I32 = mybir.dt.int32
U32 = mybir.dt.uint32
U16 = mybir.dt.uint16
U8 = mybir.dt.uint8
FP8X4 = mybir.dt.float8_e4m3fn_x4
FP4X4 = mybir.dt.float4_e2m1fn_x4
COPY = mybir.ActivationFunctionType.Copy
ADD = mybir.AluOpType.add
MULT = mybir.AluOpType.mult
MAX = mybir.AluOpType.max

P = 128
PACK = 4
RUN = 8
HALVES = Q // P
LIST_COLS = I // 16


def dealt(ap):
    return ap.rearrange("p (b t r) -> p t b r", t=PACK, r=RUN)


def tile_attend_passedthrough_mergedvalues_lean_pl_kernel(
    tc, query, keys_words, keys_scales, w_factor, vals, vals2, v_factor, offs, offs2, offs3, offs4, out_0, out_1, out_2
):
    nc = tc.nc
    with ExitStack() as ctx:
        keep = ctx.enter_context(tc.tile_pool(name="keep", bufs=1))
        psum = ctx.enter_context(tc.psum_pool(name="psum", bufs=1))

        def tile(name, shape, dtype, tag=None):
            return keep.tile(shape, dtype, name=name, tag=tag or name, align_bytes=64)

        key_list = tile("key_list", [P, LIST_COLS], U16)
        put_list = tile("put_list", [P, LIST_COLS], U16)
        get_list = tile("get_list", [P, LIST_COLS], U16)
        second_list = tile("second_list", [P, LIST_COLS], U16)
        pool_words = tile("pool_words", [P, T], U16)
        pool_scales = tile("pool_scales", [P, T], U8)
        q_raw = tile("q_raw", [P, PACK, Q], F32)
        first = [tile(f"first{t}", [P, T], F32) for t in range(PACK)]
        second = [tile(f"second{t}", [P, X], F32) for t in range(PACK)]
        places = [tile(f"places{h}", [P, Z], F32) for h in range(HALVES)]
        factor_in = tile("factor_in", [2, I], F32)
        factor_rows = tile("factor_rows", [P, PACK, P], F32)
        factors = tile("factors", [P, 2, PACK], F32)
        ident = tile("ident", [P, P], F32)

        nc.gpsimd.memset(pool_scales[:].bitcast(I32), 0)
        for h in range(HALVES):
            nc.vector.memset(places[h][:], 0.0)
        nc.vector.memset(factor_rows[:], 0.0)
        for n, vec in enumerate((w_factor, v_factor)):
            nc.scalar.dma_start(out=factor_in[n : n + 1, :], in_=vec)
        make_identity(nc, ident[:])

        vals_rows = vals.rearrange("(p t) c -> p t c", t=PACK)
        vals2_rows = vals2.rearrange("(p t) c -> p t c", t=PACK)
        nc.sync.dma_start(key_list[:], offs)
        nc.sync.dma_start(out=pool_words[:].bitcast(I32), in_=keys_words[0].bitcast(I32))
        for quad in range(4):
            nc.sync.dma_start(
                out=pool_scales[32 * quad : 32 * quad + 4, :].bitcast(I32),
                in_=keys_scales[0, 4 * quad : 4 * quad + 4, :].bitcast(I32),
            )
        nc.sync.dma_start(second_list[:], offs4)
        nc.sync.dma_start(out=q_raw[:], in_=query.rearrange("(p j) q -> p j q", j=PACK))
        nc.sync.dma_start(out=second[0][:], in_=vals2_rows[:, 0, :])
        nc.sync.dma_start(out=second[1][:], in_=vals2_rows[:, 1, :])
        nc.sync.dma_start(put_list[:], offs2)
        nc.sync.dma_start(out=first[0][:], in_=vals_rows[:, 0, :])
        nc.sync.dma_start(get_list[:], offs3)
        nc.sync.dma_start(out=first[1][:], in_=vals_rows[:, 1, :])
        nc.sync.dma_start(out=second[2][:], in_=vals2_rows[:, 2, :])
        for t in (2, 3):
            nc.sync.dma_start(out=first[t][:], in_=vals_rows[:, t, :])
        nc.sync.dma_start(out=second[3][:], in_=vals2_rows[:, 3, :])

        def turn(name, tag, src, bufs):
            bank = psum.tile([P, PACK, P], F32, name=name, tag=tag, bufs=bufs)
            for t in range(PACK):
                nc.tensor.transpose(bank[:, t, :], src[:, t, :], ident[:])
            return bank

        nc.vector.tensor_copy(factor_rows[0:2].rearrange("p t (b r) -> p t b r", r=RUN), dealt(factor_in[:]))
        factor_bank = turn("factor_bank", "factor_bank", factor_rows, 1)
        nc.scalar.activation(factors[:], factor_bank[:, :, 0:2].rearrange("p t n -> p n t"), COPY)

        key_scales = tile("key_scales", [P, I], U8)
        key_words = tile("key_words", [P, I], U16)
        nc.vector.tensor_copy(key_scales[:], pool_scales[:].indirect(key_list[:]))
        nc.vector.tensor_copy(key_words[:], pool_words[:].indirect(key_list[:]))

        def quantise(name, src, width):
            codes = tile(name + "_codes", [P, width], U32)
            scales = tile(name + "_scales", [P, width], U8)
            nc.vector.quantize_mx(out=codes[:].bitcast(FP8X4), scales=scales[:], in_=src)
            return codes, scales

        score_banks, scores = [], []
        for h in range(HALVES):
            q_bf = tile(f"q_bf{h}", [P, P, PACK], BF16)
            nc.scalar.activation(q_bf[:], q_raw[:, :, P * h : P * (h + 1)].rearrange("p t q -> p q t"), COPY)
            q_codes, q_scales = quantise(f"q{h}", q_bf[:].rearrange("p q t -> p (q t)"), P)
            bank = psum.tile([P, I], F32, name=f"score_bank{h}", tag=f"half{h}")
            nc.tensor.matmul_mx(
                out=bank[:],
                lhsT=q_codes[:].bitcast(FP8X4),
                lhsT_scale=q_scales[:],
                rhs=key_words[:].bitcast(FP4X4),
                rhs_scale=key_scales[:],
                start=True,
                stop=True,
            )
            score_banks.append(bank)

        first_g = [tile(f"first_g{t}", [P, I], F32) for t in range(PACK)]
        second_g = [tile(f"second_g{t}", [P, I], F32, "q_raw" if t == 1 else None) for t in range(PACK)]

        def gather_scalar(dst, window, offsets):
            nc.scalar.activation(dst[:], window[:].indirect(offsets[:]), COPY)

        def gather_vector(dst, window, offsets):
            nc.vector.tensor_copy(dst[:], window[:].indirect(offsets[:]))

        gather_scalar(second_g[0], second[0], second_list)
        gather_vector(second_g[1], second[1], second_list)

        for h in range(HALVES):
            score = tile(f"score{h}", [P, I], F32)
            nc.scalar.copy(score[:], score_banks[h][:])
            scores.append(score)

        nc.vector.tensor_copy(places[0][:].indirect(put_list[:]), scores[0][:])
        for part in range(2):
            nc.scalar.activation(
                places[1][:].indirect(put_list[:, 16 * part : 16 * (part + 1)]),
                scores[1][:, 256 * part : 256 * (part + 1)],
                COPY,
            )

        looked = [tile(f"looked{h}", [P, I], F32) for h in range(HALVES)]
        gather_vector(first_g[0], first[0], key_list)
        gather_scalar(looked[0], places[0], get_list)
        gather_vector(looked[1], places[1], get_list)

        def scale_round(rounded, bank, column):
            nc.vector.tensor_tensor(
                rounded,
                bank[:].rearrange("p t c -> p c t"),
                factors[:, column : column + 1, :].to_broadcast([P, P, PACK]),
                MULT,
            )
            return rounded

        def merge(t, merged, parts=1):
            step = PACK // parts
            for j in range(0, PACK, step):
                nc.vector.tensor_tensor(
                    merged[:, j : j + step, :].rearrange("p t (b r) -> p t b r", r=RUN),
                    dealt(first_g[t][:])[:, j : j + step],
                    dealt(second_g[t][:])[:, j : j + step],
                    MAX,
                )
            return turn(f"v_bank{t}", "v_bank", merged, 3)

        def fresh(name, tag=None):
            return tile(name, [P, PACK, P], F32, tag)[:]

        def fresh_bf(name, tag=None):
            return tile(name, [P, P, PACK], BF16, tag)[:]

        pair = tile("pair", [P, 2, PACK, P], F32, "places0")
        v_banks = [merge(0, pair[:, 0])]
        w_banks = []
        for h in range(HALVES):
            weights = fresh("weights0") if h == 0 else pair[:, 1]
            nc.vector.tensor_tensor(
                weights.rearrange("p t (b r) -> p t b r", r=RUN), dealt(looked[h][:]), dealt(score_banks[h][:]), ADD
            )
            w_banks.append(turn(f"w_bank{h}", f"half{h}", weights, 1))

        v_bf = [scale_round(fresh_bf("v_bf0"), v_banks[0], 1)]
        w_bf = [scale_round(fresh_bf(f"w_bf{h}"), w_banks[h], 0) for h in range(HALVES)]
        gather_scalar(first_g[1], first[1], key_list)
        v_banks.append(merge(1, fresh("merged1")))
        w_q = [quantise(f"w{h}", w_bf[h].rearrange("p q t -> p (q t)"), P) for h in range(HALVES)]

        out_banks = [psum.tile([P, PACK, P], F32, name=f"out_bank{h}") for h in range(HALVES)]

        def product(t):
            v_codes, v_scales = quantise(f"v{t}", v_bf[t].rearrange("p e t -> p (e t)"), P)
            for h in range(HALVES):
                nc.tensor.matmul_mx(
                    out=out_banks[h][:, t, :],
                    lhsT=v_codes[:].bitcast(FP8X4),
                    lhsT_scale=v_scales[:],
                    rhs=w_q[h][0][:].bitcast(FP8X4),
                    rhs_scale=w_q[h][1][:],
                    start=True,
                    stop=True,
                )

        product(0)
        gather_scalar(second_g[2], second[2], second_list)
        gather_scalar(first_g[2], first[2], key_list)
        v_banks.append(merge(2, fresh("merged2")))
        v_bf.append(scale_round(fresh_bf("v_bf1", "first2"), v_banks[1], 1))
        product(1)
        gather_scalar(first_g[3], first[3], key_list)
        gather_scalar(second_g[3], second[3], second_list)

        late = tile("late", [P, X], F32, "second3")
        early_rows = late[:, 0 : 2 * Q].rearrange("p (t q) -> p t q", t=2)
        late_bf = late[:, 2 * Q : 3 * Q].bitcast(BF16).rearrange("p (e t) -> p e t", t=PACK)
        last_rows = tile("last_rows", [P, 2, Q], F32)
        out_rows = out_0.rearrange("(p t) q -> p t q", t=PACK)
        for h in range(HALVES):
            nc.scalar.copy(early_rows[:, :, P * h : P * (h + 1)], out_banks[h][:, 0:2, :])
        nc.sync.dma_start(out=out_rows[:, 0:2, :], in_=early_rows)

        v_banks.append(merge(3, fresh("merged3"), 2))
        v_bf.append(scale_round(late_bf, v_banks[2], 1))
        product(2)
        v_bf.append(scale_round(fresh_bf("v_bf3"), v_banks[3], 1))
        product(3)

        out_bf = [tile(f"out_bf{h}", [P, P, PACK], BF16) for h in range(HALVES)]
        nc.vector.tensor_copy(out_bf[0][:], out_banks[0][:].rearrange("p t q -> p q t"))
        nc.scalar.copy(out_bf[1][:], out_banks[1][:].rearrange("p t q -> p q t"))
        out_codes = tile("out_codes", [P, Q], U32)
        out_scales = tile("out_scales", [P, Q], U8)
        for h in range(HALVES):
            cols = slice(P * h, P * (h + 1))
            nc.vector.quantize_mx(
                out=out_codes[:, cols].bitcast(FP8X4),
                scales=out_scales[:, cols],
                in_=out_bf[h][:].rearrange("p q t -> p (q t)"),
            )
        for h in (1, 0):
            nc.scalar.copy(last_rows[:, :, P * h : P * (h + 1)], out_banks[h][:, 2:4, :])
        nc.scalar.dma_start(out=out_rows[:, 2:4, :], in_=last_rows[:])
        nc.sync.dma_start(
            out=out_1[0].rearrange("p c r -> p (c r)").bitcast(I32), in_=out_codes[:].bitcast(I32)
        )
        for quad in range(4):
            queue = nc.sync if quad < 2 else nc.scalar
            queue.dma_start(
                out=out_2[0, 4 * quad : 4 * quad + 4, :].bitcast(I32),
                in_=out_scales[32 * quad : 32 * quad + 4, :].bitcast(I32),
            )
